import numpy as np
import ml_dtypes


def mxq(x, axis, fmt="e4m3"):
    dtype, down = {"e4m3": (ml_dtypes.float8_e4m3fn, 7), "e5m2": (ml_dtypes.float8_e5m2, 14)}[fmt]
    v = np.moveaxis(np.asarray(x, np.float32).astype(ml_dtypes.bfloat16).astype(np.float64), axis, -1)
    blocks = v.reshape(v.shape[:-1] + (-1, 32))
    amax = np.abs(blocks).max(-1, keepdims=True)
    byte = np.maximum(np.where(amax > 0, np.frexp(amax)[1] - 1 + 127, 0) - down, 1)
    scale = np.exp2(byte - 127.0)
    codes = (blocks / scale).astype(np.float32).astype(dtype).astype(np.float64)
    return np.moveaxis((codes * scale).reshape(v.shape), -1, axis)


WIDE = False


def mx_kscale(k):
    if not WIDE:
        return np.ones(k)
    levels = np.array([10, -10, 5, -5, 0])
    if k % 512:
        return np.exp2(np.random.permutation(np.resize(levels, k // 32))).repeat(32)
    a = np.empty((k // 512, 16))
    for p in range(k // 512):
        a[p, :8] = np.random.permutation(np.resize(levels, 8))
        for g in range(8):
            far = levels[np.abs(levels - a[p, g]) >= 10]
            a[p, g + 8] = far[np.random.randint(len(far))]
    return np.exp2(a.ravel()).repeat(32)


def f64(x):
    return np.asarray(x).astype(np.float64)


def striped(idx):
    return np.tile(idx.reshape(-1, 16).T, (8, 1)).astype(np.uint16)


def unstriped(offs):
    return offs[:16].T.reshape(-1).astype(np.int64)


def pack_weight(w):
    k, n = w.shape
    w = f64(np.asarray(w, np.float32).astype(ml_dtypes.bfloat16)).reshape(k // 32, 32, n)
    amax = np.abs(w).max(1)
    byte = np.clip(np.where(amax > 0, np.frexp(amax)[1] - 1 + 127 - 7, 1), 1, 254)
    scaled = (w * np.exp2(127.0 - byte)[:, None, :]).reshape(k, n).astype(np.float32)
    words = np.ascontiguousarray(scaled.reshape(k // 512, 128, 4, n).transpose(0, 1, 3, 2)).astype(ml_dtypes.float8_e4m3fn).view(np.uint8)
    return words, np.ascontiguousarray(byte.astype(np.uint8).reshape(k // 512, 16, n))


def unpack_weight(words, scales):
    g, p, n, _ = words.shape
    vals = np.ascontiguousarray(words).view(ml_dtypes.float8_e4m3fn).astype(np.float64) * np.repeat(np.exp2(scales.astype(np.float64) - 127.0), 8, axis=1)[..., None]
    return vals.transpose(0, 1, 3, 2).reshape(g * 512, n)


E2M1 = np.array([0.0, 0.5, 1.0, 1.5, 2.0, 3.0, 4.0, 6.0, -0.0, -0.5, -1.0, -1.5, -2.0, -3.0, -4.0, -6.0])


def pack_fp4(w):
    k, n = w.shape
    w = f64(np.asarray(w, np.float32).astype(ml_dtypes.bfloat16)).reshape(k // 32, 32, n)
    amax = np.abs(w).max(1)
    mant, ex = np.frexp(amax / 6.0)
    byte = np.clip(np.where(amax > 0, np.where(mant > 0.5, ex, ex - 1) + 127, 1), 1, 254)
    scaled = (w * np.exp2(127.0 - byte)[:, None, :]).reshape(k, n).astype(np.float32)
    c = np.ascontiguousarray(scaled.reshape(k // 512, 128, 4, n).transpose(0, 1, 3, 2)).astype(ml_dtypes.float4_e2m1fn).view(np.uint8) & 0xF
    words = (c[..., 0::2] | (c[..., 1::2] << 4)).reshape(k // 512, 128, 2 * n)
    return np.ascontiguousarray(words), np.ascontiguousarray(byte.astype(np.uint8).reshape(k // 512, 16, n))


def unpack_fp4(words, scales):
    g, _, n = scales.shape
    words = np.ascontiguousarray(words).reshape(g, 128, n, 2)
    nib = np.empty((g, 128, n, 4), np.uint8)
    nib[..., 0::2] = words & 0xF
    nib[..., 1::2] = words >> 4
    vals = E2M1[nib] * np.repeat(np.exp2(scales.astype(np.float64) - 127.0), 8, axis=1)[..., None]
    return vals.transpose(0, 1, 3, 2).reshape(g * 512, n)


def relu(v):
    return np.maximum(v, 0.0)

def planes(y):
    n, m = y.shape
    v = y.astype(np.float32).astype(ml_dtypes.bfloat16).astype(np.float64).reshape(n // 32, 32, m)
    top = np.abs(v).max(1)
    byte = np.clip(np.where(top > 0, np.frexp(top)[1] - 1 + 127 - 7, 1), 1, 254)
    codes = (v * np.exp2(127.0 - byte)[:, None, :]).reshape(n, m).astype(np.float32).astype(ml_dtypes.float8_e4m3fn).view(np.uint8)
    words = codes.reshape(n // 512, 128, 4, m).transpose(0, 1, 3, 2)
    return np.ascontiguousarray(words), np.ascontiguousarray(byte.astype(np.uint8).reshape(n // 512, 16, m))


K, T, S, H, C = 512, 2048, 256, 512, 512


def setup_inputs():
    n = np.random.standard_normal
    s = mx_kscale(K)[:, None]
    packed_xT = pack_weight(n((K, T)) * s)
    packed_w1 = pack_fp4(n((K, H)) / np.sqrt(K) / s)
    return {
        "x_words": packed_xT[0],
        "x_scales": packed_xT[1],
        "w1_words": packed_w1[0],
        "w1_scales": packed_w1[1],
        "gs": (np.random.uniform(0.5, 1.5, (K, 1)) / s).astype(np.float32),
        "offs": striped(np.random.permutation(T)[:S]),
        "n1": striped(np.random.permutation(S)),
        "n2": striped(np.random.permutation(S)),
        "cand": striped(np.random.permutation(T)[:C]),
        "n3": striped(np.random.permutation(S)),
    }


def reference(x_words, x_scales, w1_words, w1_scales, gs, offs, n1, n2, cand, n3):
    x_cand = unpack_weight(x_words, x_scales)[:, unstriped(cand)]
    xq = unpack_weight(x_words, x_scales)[:, unstriped(offs)]
    y = unpack_fp4(w1_words, w1_scales).T @ xq
    z = f64(gs) * (y - (np.minimum(y[:, unstriped(n1)], y[:, unstriped(n2)])))
    s = 0.0625 * ((x_cand.T @ mxq(z, 0, "e4m3")))
    rl = relu(s)
    ds = np.zeros((C, S))
    ds[:, unstriped(n3)] = rl
    out_0 = ds - (0.5 * s)
    return (out_0,) + planes(out_0)

@@ -1,0 +1,158 @@
+from contextlib import ExitStack
+
+import concourse.mybir as mybir
+
+K, T, S, H, C = 512, 2048, 256, 512, 512
+FLOPS = 2 * K * H * S + 2 * K * C * S
+BYTES = (K * (S + C) + K * (S + C) // 32) + K * H // 2 + K * H // 32 + 4 * K + C * S * 4 + C * S + C * S // 32
+
+F32 = mybir.dt.float32
+BF16 = mybir.dt.bfloat16
+I32 = mybir.dt.int32
+U32 = mybir.dt.uint32
+U16 = mybir.dt.uint16
+U8 = mybir.dt.uint8
+FP8X4 = mybir.dt.float8_e4m3fn_x4
+FP4X4 = mybir.dt.float4_e2m1fn_x4
+ALU = mybir.AluOpType
+ACT = mybir.ActivationFunctionType
+COPY = ACT.Copy
+
+P = 128
+PACK = 4
+HALF = S // 2
+LIST_ROWS = 16
+
+
+def entries(list_tile, first, count):
+    return list_tile[:, first // LIST_ROWS : (first + count) // LIST_ROWS]
+
+
+def tile_picked_candundersend_none_po_kernel(tc, x_words, x_scales, w1_words, w1_scales, gs, offs, n1, n2, cand, n3, out_0, out_1, out_2):
+    nc = tc.nc
+    with ExitStack() as ctx:
+        sb = ctx.enter_context(tc.tile_pool(name="sb", bufs=1))
+        ps = ctx.enter_context(tc.psum_pool(name="ps", bufs=1))
+
+        offs_t = sb.tile([P, S // LIST_ROWS], U16, name="offs_t")
+        cand_t = sb.tile([P, C // LIST_ROWS], U16, name="cand_t")
+        n1_t = sb.tile([P, S // LIST_ROWS], U16, name="n1_t")
+        n2_t = sb.tile([P, S // LIST_ROWS], U16, name="n2_t")
+        n3_t = sb.tile([P, S // LIST_ROWS], U16, name="n3_t")
+        xw = sb.tile([P, T], U32, name="xw", align_bytes=64)
+        xs = sb.tile([P, T], U8, name="xs", align_bytes=64)
+        ww_raw = sb.tile([P, H], U16, name="ww_raw", align_bytes=64)
+        ws_raw = sb.tile([P, H], U8, name="ws_raw", align_bytes=64)
+        gs_t = sb.tile([P, PACK], F32, name="gs_t")
+
+        nc.vector.memset(xs[:].bitcast(I32), 0)
+        nc.gpsimd.memset(ws_raw[:].bitcast(I32), 0)
+        nc.sync.dma_start(offs_t[:], offs)
+        nc.scalar.dma_start(ww_raw[:].bitcast(I32), w1_words[0].bitcast(I32))
+        nc.scalar.dma_start(gs_t[:], gs.rearrange("(p t) o -> p (t o)", t=PACK))
+        nc.scalar.dma_start(xs[0:4, :].bitcast(I32), x_scales[0, 0:4, :].bitcast(I32))
+        nc.scalar.dma_start(xs[32:36, :].bitcast(I32), x_scales[0, 4:8, :].bitcast(I32))
+        nc.scalar.dma_start(xs[64:68, :].bitcast(I32), x_scales[0, 8:12, :].bitcast(I32))
+        nc.scalar.dma_start(xs[96:100, :].bitcast(I32), x_scales[0, 12:16, :].bitcast(I32))
+        nc.gpsimd.dma_start(ws_raw[96:100, :].bitcast(I32), w1_scales[0, 12:16, :].bitcast(I32))
+        nc.sync.dma_start(ws_raw[0:4, :].bitcast(I32), w1_scales[0, 0:4, :].bitcast(I32))
+        nc.sync.dma_start(ws_raw[32:36, :].bitcast(I32), w1_scales[0, 4:8, :].bitcast(I32))
+        nc.sync.dma_start(ws_raw[64:68, :].bitcast(I32), w1_scales[0, 8:12, :].bitcast(I32))
+        nc.sync.dma_start(cand_t[:], cand)
+        nc.sync.dma_start(n1_t[:], n1)
+        nc.sync.dma_start(n2_t[:], n2)
+        nc.sync.dma_start(n3_t[:], n3)
+        nc.sync.dma_start(xw[:].bitcast(I32), x_words[0].rearrange("p n t -> p (n t)").bitcast(I32))
+
+        ww = sb.tile([P, PACK, P], U16, name="ww", align_bytes=64)
+        ws = sb.tile([P, PACK, P], U8, name="ws", align_bytes=64)
+        nc.scalar.copy(ww[:].rearrange("p t m -> p m t"), ww_raw[:].rearrange("p (m t) -> p m t", t=PACK))
+        gs_abs = sb.tile([P, PACK], F32, name="gs_abs")
+        gs_sign = sb.tile([P, PACK], BF16, name="gs_sign")
+        nc.scalar.activation(gs_abs[:], gs_t[:], ACT.Abs)
+        nc.scalar.activation(gs_sign[:], gs_t[:], ACT.Sign)
+        qs = sb.tile([P, S], U8, name="qs", tag="picked_scales", align_bytes=64)
+        nc.vector.tensor_copy(qs[:], xs[:].indirect(offs_t[:]))
+        nc.vector.tensor_copy(ws[:].rearrange("p t m -> p m t"), ws_raw[:].rearrange("p (m t) -> p m t", t=PACK))
+        cs = sb.tile([P, PACK, P], U8, name="cs", align_bytes=64)
+        qw = sb.tile([P, S], U32, name="qw", align_bytes=64)
+        nc.vector.tensor_copy(qw[:], xw[:].indirect(offs_t[:]))
+
+        y_ps = [ps.tile([P, S], F32, name=f"y_ps{t}") for t in range(PACK)]
+        for t in range(PACK):
+            nc.tensor.matmul_mx(y_ps[t][:], lhsT=ww[:, t, :].bitcast(FP4X4), lhsT_scale=ws[:, t, :],
+                                rhs=qw[:].bitcast(FP8X4), rhs_scale=qs[:], start=True, stop=True)
+
+        y = sb.tile([P, PACK, S], F32, name="y", align_bytes=64)
+        cw_raw = sb.tile([P, C], U32, name="cw_raw", align_bytes=64)
+        cw = sb.tile([P, PACK, P], U32, name="cw", align_bytes=64)
+        for t in range(PACK - 1):
+            nc.scalar.activation(y[:, t, :], y_ps[t][:], COPY, scale=gs_abs[:, t : t + 1])
+        nc.vector.tensor_scalar(y[:, PACK - 1, :], y_ps[PACK - 1][:], gs_abs[:, PACK - 1 : PACK], None, ALU.mult)
+        for h in range(2):
+            nc.vector.tensor_copy(cw_raw[:, S * h : S * (h + 1)], xw[:].indirect(entries(cand_t, S * h, S)))
+        nc.vector.tensor_copy(cw[:].rearrange("p t m -> p m t"), cw_raw[:].rearrange("p (m t) -> p m t", t=PACK))
+        cs_raw = sb.tile([P, C], U8, name="cs_raw", tag="picked_scales", align_bytes=64)
+        nc.vector.tensor_copy(cs_raw[:], xs[:].indirect(cand_t[:]))
+        nc.vector.tensor_copy(cs[:].rearrange("p t m -> p m t"), cs_raw[:].rearrange("p (m t) -> p m t", t=PACK))
+
+        s_ps = [ps.tile([P, S], F32, name=f"s_ps{t}") for t in range(PACK)]
+        ds = [sb.tile([P, S], F32, name=f"ds{t}", align_bytes=64) for t in range(PACK)]
+        rl = sb.tile([P, PACK, S], F32, name="rl", align_bytes=64)
+        sign_b = gs_sign[:].unsqueeze(1).to_broadcast([P, HALF, PACK])
+        g1 = sb.tile([P, PACK, HALF], F32, name="g1", align_bytes=64)
+        g2 = sb.tile([P, PACK, HALF], F32, name="g2", align_bytes=64)
+
+        def gathers(h):
+            for t in range(PACK):
+                nc.scalar.activation(g1[:, t, :], y[:, t, :].indirect(entries(n1_t, HALF * h, HALF)), COPY)
+                nc.scalar.activation(g2[:, t, :], y[:, t, :].indirect(entries(n2_t, HALF * h, HALF)), COPY)
+
+        def make_z(h):
+            cols = slice(HALF * h, HALF * (h + 1))
+            low = sb.tile([P, PACK, HALF], F32, name=f"low{h}", tag=("low", "zb_then_low")[h], align_bytes=64)
+            za = sb.tile([P, HALF * PACK], BF16, name=f"za{h}", tag=("za", "zw_then_za")[h], align_bytes=64)
+            zb = sb.tile([P, HALF * PACK], BF16, name=f"zb{h}", tag=("zb_then_low", "zb")[h], align_bytes=64)
+            zw = sb.tile([P, HALF], U32, name=f"zw{h}", tag=("zw_then_za", "zw")[h], align_bytes=64)
+            zs = sb.tile([P, HALF], U8, name=f"zs{h}", align_bytes=64)
+            for planes in (slice(0, PACK - 1), slice(PACK - 1, PACK)):
+                nc.vector.tensor_tensor(low[:, planes, :], g1[:, planes, :], g2[:, planes, :], ALU.min)
+            nc.vector.tensor_tensor(za[:].rearrange("p (c i t) -> p c t i", i=2, t=PACK),
+                                    y[:, :, cols].rearrange("p t (c i) -> p c t i", i=2),
+                                    low[:].rearrange("p t (c i) -> p c t i", i=2), ALU.subtract)
+            nc.vector.tensor_tensor(zb[:].rearrange("p (j t) -> p j t", t=PACK), za[:].rearrange("p (j t) -> p j t", t=PACK), sign_b, ALU.mult)
+            nc.vector.quantize_mx(zw[:].bitcast(FP8X4), zs[:], zb[:])
+            for t in range(PACK):
+                nc.tensor.matmul_mx(s_ps[t][:, cols], lhsT=cw[:, t, :].bitcast(FP8X4), lhsT_scale=cs[:, t, :],
+                                    rhs=zw[:].bitcast(FP8X4), rhs_scale=zs[:], start=True, stop=True)
+            for t in range(PACK):
+                nc.vector.tensor_scalar(rl[:, t, cols], s_ps[t][:, cols], 0.0625, 0.0, ALU.mult, ALU.max)
+
+        def scatter(h, t):
+            cols = slice(HALF * h, HALF * (h + 1))
+            nc.scalar.activation(ds[t][:].indirect(entries(n3_t, HALF * h, HALF)), rl[:, t, cols], COPY)
+
+        res = sb.tile([P, PACK, S], F32, name="res", align_bytes=64)
+        rb = sb.tile([P, S * PACK], BF16, name="rb", align_bytes=64)
+        ow = sb.tile([P, S], U32, name="ow", align_bytes=64)
+        osc = sb.tile([P, S], U8, name="osc", align_bytes=64)
+        out_rows = out_0.rearrange("(p t) j -> p t j", t=PACK)
+
+        gathers(0)
+        make_z(0)
+        gathers(1)
+        for t in range(PACK):
+            scatter(0, t)
+        make_z(1)
+        for t in range(PACK):
+            scatter(1, t)
+            nc.vector.scalar_tensor_tensor(res[:, t, :], s_ps[t][:], -0.03125, ds[t][:], ALU.mult, ALU.add)
+            nc.sync.dma_start(out_rows[:, t, :], res[:, t, :])
+            if t % 2 == 1:
+                nc.vector.tensor_copy(rb[:].rearrange("p (j t) -> p j t", t=PACK)[:, :, t - 1 : t + 1],
+                                      res[:, t - 1 : t + 1, :].rearrange("p t j -> p j t"))
+        nc.vector.quantize_mx(ow[:].bitcast(FP8X4), osc[:], rb[:])
+        nc.scalar.dma_start(out_1[0].rearrange("p n t -> p (n t)").bitcast(I32), ow[:].bitcast(I32))
+        for q in range(4):
+            eng = nc.sync if q % 2 == 0 else nc.scalar
+            eng.dma_start(out_2[0, 4 * q : 4 * q + 4, :].bitcast(I32), osc[32 * q : 32 * q + 4, :].bitcast(I32))

@@ -42,27 +42,28 @@ def tile_picked_candundersend_none_po_kernel(tc, x_words, x_scales, w1_words, w1
         xw = sb.tile([P, T], U32, name="xw", align_bytes=64)
         xs = sb.tile([P, T], U8, name="xs", align_bytes=64)
         ww_raw = sb.tile([P, H], U16, name="ww_raw", align_bytes=64)
-        ws_raw = sb.tile([P, H], U8, name="ws_raw", align_bytes=64)
+        ws_raw = sb.tile([P, H], U8, name="ws_raw", tag="ws_raw_then_cw_raw", align_bytes=64)
         gs_t = sb.tile([P, PACK], F32, name="gs_t")
 
-        nc.vector.memset(xs[:].bitcast(I32), 0)
-        nc.gpsimd.memset(ws_raw[:].bitcast(I32), 0)
+        nc.vector.memset(xs[:, : T // 2].bitcast(I32), 0)
+        nc.gpsimd.memset(xs[:, T // 2 :].bitcast(I32), 0)
+        nc.vector.memset(ws_raw[:].bitcast(I32), 0)
         nc.sync.dma_start(offs_t[:], offs)
-        nc.scalar.dma_start(ww_raw[:].bitcast(I32), w1_words[0].bitcast(I32))
-        nc.scalar.dma_start(gs_t[:], gs.rearrange("(p t) o -> p (t o)", t=PACK))
-        nc.scalar.dma_start(xs[0:4, :].bitcast(I32), x_scales[0, 0:4, :].bitcast(I32))
-        nc.scalar.dma_start(xs[32:36, :].bitcast(I32), x_scales[0, 4:8, :].bitcast(I32))
-        nc.scalar.dma_start(xs[64:68, :].bitcast(I32), x_scales[0, 8:12, :].bitcast(I32))
-        nc.scalar.dma_start(xs[96:100, :].bitcast(I32), x_scales[0, 12:16, :].bitcast(I32))
-        nc.gpsimd.dma_start(ws_raw[96:100, :].bitcast(I32), w1_scales[0, 12:16, :].bitcast(I32))
+        nc.sync.dma_start(cand_t[:], cand)
+        nc.sync.dma_start(ww_raw[:].bitcast(I32), w1_words[0].bitcast(I32))
+        nc.sync.dma_start(xs[0:4, :].bitcast(I32), x_scales[0, 0:4, :].bitcast(I32))
+        nc.sync.dma_start(xs[32:36, :].bitcast(I32), x_scales[0, 4:8, :].bitcast(I32))
+        nc.sync.dma_start(xs[64:68, :].bitcast(I32), x_scales[0, 8:12, :].bitcast(I32))
+        nc.sync.dma_start(xs[96:100, :].bitcast(I32), x_scales[0, 12:16, :].bitcast(I32))
+        nc.sync.dma_start(xw[:].bitcast(I32), x_words[0].rearrange("p n t -> p (n t)").bitcast(I32))
         nc.sync.dma_start(ws_raw[0:4, :].bitcast(I32), w1_scales[0, 0:4, :].bitcast(I32))
         nc.sync.dma_start(ws_raw[32:36, :].bitcast(I32), w1_scales[0, 4:8, :].bitcast(I32))
         nc.sync.dma_start(ws_raw[64:68, :].bitcast(I32), w1_scales[0, 8:12, :].bitcast(I32))
-        nc.sync.dma_start(cand_t[:], cand)
+        nc.sync.dma_start(ws_raw[96:100, :].bitcast(I32), w1_scales[0, 12:16, :].bitcast(I32))
+        nc.sync.dma_start(gs_t[:], gs.rearrange("(p t) o -> p (t o)", t=PACK))
         nc.sync.dma_start(n1_t[:], n1)
         nc.sync.dma_start(n2_t[:], n2)
         nc.sync.dma_start(n3_t[:], n3)
-        nc.sync.dma_start(xw[:].bitcast(I32), x_words[0].rearrange("p n t -> p (n t)").bitcast(I32))
 
         ww = sb.tile([P, PACK, P], U16, name="ww", align_bytes=64)
         ws = sb.tile([P, PACK, P], U8, name="ws", align_bytes=64)
@@ -71,12 +72,17 @@ def tile_picked_candundersend_none_po_kernel(tc, x_words, x_scales, w1_words, w1
         gs_sign = sb.tile([P, PACK], BF16, name="gs_sign")
         nc.scalar.activation(gs_abs[:], gs_t[:], ACT.Abs)
         nc.scalar.activation(gs_sign[:], gs_t[:], ACT.Sign)
-        qs = sb.tile([P, S], U8, name="qs", tag="picked_scales", align_bytes=64)
+        qs = sb.tile([P, S], U8, name="qs", align_bytes=64)
         nc.vector.tensor_copy(qs[:], xs[:].indirect(offs_t[:]))
-        nc.vector.tensor_copy(ws[:].rearrange("p t m -> p m t"), ws_raw[:].rearrange("p (m t) -> p m t", t=PACK))
+        ws_cols = ws_raw[:].rearrange("p (m t) -> p m t", t=PACK)
+        nc.vector.tensor_copy(ws[:, 0, :], ws_cols[:, :, 0])
+        nc.vector.tensor_copy(ws[:, 1:, :].rearrange("p t m -> p m t"), ws_cols[:, :, 1:])
         cs = sb.tile([P, PACK, P], U8, name="cs", align_bytes=64)
         qw = sb.tile([P, S], U32, name="qw", align_bytes=64)
         nc.vector.tensor_copy(qw[:], xw[:].indirect(offs_t[:]))
+        cs_raw = sb.tile([P, C], U8, name="cs_raw", align_bytes=64)
+        nc.vector.tensor_copy(cs_raw[:], xs[:].indirect(cand_t[:]))
+        nc.vector.tensor_copy(cs[:].rearrange("p t m -> p m t"), cs_raw[:].rearrange("p (m t) -> p m t", t=PACK))
 
         y_ps = [ps.tile([P, S], F32, name=f"y_ps{t}") for t in range(PACK)]
         for t in range(PACK):
@@ -84,17 +90,14 @@ def tile_picked_candundersend_none_po_kernel(tc, x_words, x_scales, w1_words, w1
                                 rhs=qw[:].bitcast(FP8X4), rhs_scale=qs[:], start=True, stop=True)
 
         y = sb.tile([P, PACK, S], F32, name="y", align_bytes=64)
-        cw_raw = sb.tile([P, C], U32, name="cw_raw", align_bytes=64)
+        cw_raw = sb.tile([P, C], U32, name="cw_raw", tag="ws_raw_then_cw_raw", align_bytes=64)
         cw = sb.tile([P, PACK, P], U32, name="cw", align_bytes=64)
-        for t in range(PACK - 1):
-            nc.scalar.activation(y[:, t, :], y_ps[t][:], COPY, scale=gs_abs[:, t : t + 1])
-        nc.vector.tensor_scalar(y[:, PACK - 1, :], y_ps[PACK - 1][:], gs_abs[:, PACK - 1 : PACK], None, ALU.mult)
+        nc.scalar.activation(y[:, 0, :], y_ps[0][:], COPY, scale=gs_abs[:, 0:1])
+        for t in range(1, PACK):
+            nc.vector.tensor_scalar(y[:, t, :], y_ps[t][:], gs_abs[:, t : t + 1], None, ALU.mult)
         for h in range(2):
             nc.vector.tensor_copy(cw_raw[:, S * h : S * (h + 1)], xw[:].indirect(entries(cand_t, S * h, S)))
         nc.vector.tensor_copy(cw[:].rearrange("p t m -> p m t"), cw_raw[:].rearrange("p (m t) -> p m t", t=PACK))
-        cs_raw = sb.tile([P, C], U8, name="cs_raw", tag="picked_scales", align_bytes=64)
-        nc.vector.tensor_copy(cs_raw[:], xs[:].indirect(cand_t[:]))
-        nc.vector.tensor_copy(cs[:].rearrange("p t m -> p m t"), cs_raw[:].rearrange("p (m t) -> p m t", t=PACK))
 
         s_ps = [ps.tile([P, S], F32, name=f"s_ps{t}") for t in range(PACK)]
         ds = [sb.tile([P, S], F32, name=f"ds{t}", align_bytes=64) for t in range(PACK)]
@@ -144,14 +147,19 @@ def tile_picked_candundersend_none_po_kernel(tc, x_words, x_scales, w1_words, w1
         for t in range(PACK):
             scatter(0, t)
         make_z(1)
+        rb_cols = rb[:].rearrange("p (j t) -> p j t", t=PACK)
+        halves = [slice(HALF * h, HALF * (h + 1)) for h in range(2)]
         for t in range(PACK):
             scatter(1, t)
-            nc.vector.scalar_tensor_tensor(res[:, t, :], s_ps[t][:], -0.03125, ds[t][:], ALU.mult, ALU.add)
+            pieces = halves if t == PACK - 1 else [slice(0, S)]
+            for cols in pieces:
+                nc.vector.scalar_tensor_tensor(res[:, t, cols], s_ps[t][:, cols], -0.03125, ds[t][:, cols], ALU.mult, ALU.add)
             nc.sync.dma_start(out_rows[:, t, :], res[:, t, :])
             if t % 2 == 1:
-                nc.vector.tensor_copy(rb[:].rearrange("p (j t) -> p j t", t=PACK)[:, :, t - 1 : t + 1],
-                                      res[:, t - 1 : t + 1, :].rearrange("p t j -> p j t"))
-        nc.vector.quantize_mx(ow[:].bitcast(FP8X4), osc[:], rb[:])
+                for cols in pieces:
+                    nc.vector.tensor_copy(rb_cols[:, cols, t - 1 : t + 1], res[:, t - 1 : t + 1, cols].rearrange("p t j -> p j t"))
+        for h, cols in enumerate(halves):
+            nc.vector.quantize_mx(ow[:, cols].bitcast(FP8X4), osc[:, cols], rb[:, PACK * HALF * h : PACK * HALF * (h + 1)])
         nc.scalar.dma_start(out_1[0].rearrange("p n t -> p (n t)").bitcast(I32), ow[:].bitcast(I32))
         for q in range(4):
             eng = nc.sync if q % 2 == 0 else nc.scalar

@@ -42,7 +42,7 @@ def tile_picked_candundersend_none_po_kernel(tc, x_words, x_scales, w1_words, w1
         xw = sb.tile([P, T], U32, name="xw", align_bytes=64)
         xs = sb.tile([P, T], U8, name="xs", align_bytes=64)
         ww_raw = sb.tile([P, H], U16, name="ww_raw", align_bytes=64)
-        ws_raw = sb.tile([P, H], U8, name="ws_raw", tag="ws_raw_then_cw_raw", align_bytes=64)
+        ws_raw = sb.tile([P, H], U8, name="ws_raw", tag="ws_raw_then_cs", align_bytes=64)
         gs_t = sb.tile([P, PACK], F32, name="gs_t")
 
         nc.vector.memset(xs[:, : T // 2].bitcast(I32), 0)
@@ -53,8 +53,8 @@ def tile_picked_candundersend_none_po_kernel(tc, x_words, x_scales, w1_words, w1
         nc.sync.dma_start(ww_raw[:].bitcast(I32), w1_words[0].bitcast(I32))
         nc.sync.dma_start(xs[0:4, :].bitcast(I32), x_scales[0, 0:4, :].bitcast(I32))
         nc.sync.dma_start(xs[32:36, :].bitcast(I32), x_scales[0, 4:8, :].bitcast(I32))
-        nc.sync.dma_start(xs[64:68, :].bitcast(I32), x_scales[0, 8:12, :].bitcast(I32))
-        nc.sync.dma_start(xs[96:100, :].bitcast(I32), x_scales[0, 12:16, :].bitcast(I32))
+        nc.scalar.dma_start(xs[64:68, :].bitcast(I32), x_scales[0, 8:12, :].bitcast(I32))
+        nc.scalar.dma_start(xs[96:100, :].bitcast(I32), x_scales[0, 12:16, :].bitcast(I32))
         nc.sync.dma_start(xw[:].bitcast(I32), x_words[0].rearrange("p n t -> p (n t)").bitcast(I32))
         nc.sync.dma_start(ws_raw[0:4, :].bitcast(I32), w1_scales[0, 0:4, :].bitcast(I32))
         nc.sync.dma_start(ws_raw[32:36, :].bitcast(I32), w1_scales[0, 4:8, :].bitcast(I32))
@@ -75,31 +75,37 @@ def tile_picked_candundersend_none_po_kernel(tc, x_words, x_scales, w1_words, w1
         qs = sb.tile([P, S], U8, name="qs", align_bytes=64)
         nc.vector.tensor_copy(qs[:], xs[:].indirect(offs_t[:]))
         ws_cols = ws_raw[:].rearrange("p (m t) -> p m t", t=PACK)
-        nc.vector.tensor_copy(ws[:, 0, :], ws_cols[:, :, 0])
-        nc.vector.tensor_copy(ws[:, 1:, :].rearrange("p t m -> p m t"), ws_cols[:, :, 1:])
-        cs = sb.tile([P, PACK, P], U8, name="cs", align_bytes=64)
-        qw = sb.tile([P, S], U32, name="qw", align_bytes=64)
-        nc.vector.tensor_copy(qw[:], xw[:].indirect(offs_t[:]))
+        for t in range(PACK):
+            nc.gpsimd.tensor_copy(ws[:, t, :], ws_cols[:, :, t])
+        cs = sb.tile([P, PACK, P], U8, name="cs", tag="ws_raw_then_cs", align_bytes=64)
+        qw = sb.tile([P, S], U32, name="qw", tag="qw_then_cw_raw", align_bytes=64)
+        for h in range(2):
+            nc.vector.tensor_copy(qw[:, HALF * h : HALF * (h + 1)], xw[:].indirect(entries(offs_t, HALF * h, HALF)))
         cs_raw = sb.tile([P, C], U8, name="cs_raw", align_bytes=64)
         nc.vector.tensor_copy(cs_raw[:], xs[:].indirect(cand_t[:]))
         nc.vector.tensor_copy(cs[:].rearrange("p t m -> p m t"), cs_raw[:].rearrange("p (m t) -> p m t", t=PACK))
 
-        y_ps = [ps.tile([P, S], F32, name=f"y_ps{t}") for t in range(PACK)]
-        for t in range(PACK):
-            nc.tensor.matmul_mx(y_ps[t][:], lhsT=ww[:, t, :].bitcast(FP4X4), lhsT_scale=ws[:, t, :],
-                                rhs=qw[:].bitcast(FP8X4), rhs_scale=qs[:], start=True, stop=True)
+        pieces = [(0, slice(0, HALF), "y_first"), (0, slice(HALF, S), "y_then_s")] + [(t, slice(0, S), f"y{t}") for t in range(1, PACK)]
+        y_ps = []
+        for t, cols, tag in pieces:
+            bank = ps.tile([P, cols.stop - cols.start], F32, name=f"y_ps{t}_{cols.start}", tag=tag)
+            nc.tensor.matmul_mx(bank[:], lhsT=ww[:, t, :].bitcast(FP4X4), lhsT_scale=ws[:, t, :],
+                                rhs=qw[:, cols].bitcast(FP8X4), rhs_scale=qs[:, cols], start=True, stop=True)
+            y_ps.append(bank)
 
         y = sb.tile([P, PACK, S], F32, name="y", align_bytes=64)
-        cw_raw = sb.tile([P, C], U32, name="cw_raw", tag="ws_raw_then_cw_raw", align_bytes=64)
         cw = sb.tile([P, PACK, P], U32, name="cw", align_bytes=64)
-        nc.scalar.activation(y[:, 0, :], y_ps[0][:], COPY, scale=gs_abs[:, 0:1])
-        for t in range(1, PACK):
-            nc.vector.tensor_scalar(y[:, t, :], y_ps[t][:], gs_abs[:, t : t + 1], None, ALU.mult)
+        for (t, cols, tag), bank in zip(pieces, y_ps):
+            if t == 0:
+                nc.scalar.activation(y[:, t, cols], bank[:], COPY, scale=gs_abs[:, t : t + 1])
+            else:
+                nc.vector.tensor_scalar(y[:, t, cols], bank[:], gs_abs[:, t : t + 1], None, ALU.mult)
         for h in range(2):
-            nc.vector.tensor_copy(cw_raw[:, S * h : S * (h + 1)], xw[:].indirect(entries(cand_t, S * h, S)))
-        nc.vector.tensor_copy(cw[:].rearrange("p t m -> p m t"), cw_raw[:].rearrange("p (m t) -> p m t", t=PACK))
+            cw_raw = sb.tile([P, S], U32, name=f"cw_raw{h}", tag=("cw_raw", "qw_then_cw_raw")[h], align_bytes=64)
+            nc.vector.tensor_copy(cw_raw[:], xw[:].indirect(entries(cand_t, S * h, S)))
+            nc.vector.tensor_copy(cw[:, :, 64 * h : 64 * (h + 1)].rearrange("p t m -> p m t"), cw_raw[:].rearrange("p (m t) -> p m t", t=PACK))
 
-        s_ps = [ps.tile([P, S], F32, name=f"s_ps{t}") for t in range(PACK)]
+        s_ps = [ps.tile([P, S], F32, name=f"s_ps{t}", tag=("s0", "s1", "s2", "y_then_s")[t]) for t in range(PACK)]
         ds = [sb.tile([P, S], F32, name=f"ds{t}", align_bytes=64) for t in range(PACK)]
         rl = sb.tile([P, PACK, S], F32, name="rl", align_bytes=64)
         sign_b = gs_sign[:].unsqueeze(1).to_broadcast([P, HALF, PACK])

@@ -42,7 +42,7 @@ def tile_picked_candundersend_none_po_kernel(tc, x_words, x_scales, w1_words, w1
         xw = sb.tile([P, T], U32, name="xw", align_bytes=64)
         xs = sb.tile([P, T], U8, name="xs", align_bytes=64)
         ww_raw = sb.tile([P, H], U16, name="ww_raw", align_bytes=64)
-        ws_raw = sb.tile([P, H], U8, name="ws_raw", tag="ws_raw_then_cs", align_bytes=64)
+        ws_raw = sb.tile([P, H], U8, name="ws_raw", align_bytes=64)
         gs_t = sb.tile([P, PACK], F32, name="gs_t")
 
         nc.vector.memset(xs[:, : T // 2].bitcast(I32), 0)
@@ -53,8 +53,8 @@ def tile_picked_candundersend_none_po_kernel(tc, x_words, x_scales, w1_words, w1
         nc.sync.dma_start(ww_raw[:].bitcast(I32), w1_words[0].bitcast(I32))
         nc.sync.dma_start(xs[0:4, :].bitcast(I32), x_scales[0, 0:4, :].bitcast(I32))
         nc.sync.dma_start(xs[32:36, :].bitcast(I32), x_scales[0, 4:8, :].bitcast(I32))
-        nc.scalar.dma_start(xs[64:68, :].bitcast(I32), x_scales[0, 8:12, :].bitcast(I32))
-        nc.scalar.dma_start(xs[96:100, :].bitcast(I32), x_scales[0, 12:16, :].bitcast(I32))
+        nc.sync.dma_start(xs[64:68, :].bitcast(I32), x_scales[0, 8:12, :].bitcast(I32))
+        nc.sync.dma_start(xs[96:100, :].bitcast(I32), x_scales[0, 12:16, :].bitcast(I32))
         nc.sync.dma_start(xw[:].bitcast(I32), x_words[0].rearrange("p n t -> p (n t)").bitcast(I32))
         nc.sync.dma_start(ws_raw[0:4, :].bitcast(I32), w1_scales[0, 0:4, :].bitcast(I32))
         nc.sync.dma_start(ws_raw[32:36, :].bitcast(I32), w1_scales[0, 4:8, :].bitcast(I32))
@@ -75,15 +75,13 @@ def tile_picked_candundersend_none_po_kernel(tc, x_words, x_scales, w1_words, w1
         qs = sb.tile([P, S], U8, name="qs", align_bytes=64)
         nc.vector.tensor_copy(qs[:], xs[:].indirect(offs_t[:]))
         ws_cols = ws_raw[:].rearrange("p (m t) -> p m t", t=PACK)
-        for t in range(PACK):
-            nc.gpsimd.tensor_copy(ws[:, t, :], ws_cols[:, :, t])
-        cs = sb.tile([P, PACK, P], U8, name="cs", tag="ws_raw_then_cs", align_bytes=64)
-        qw = sb.tile([P, S], U32, name="qw", tag="qw_then_cw_raw", align_bytes=64)
+        nc.vector.tensor_copy(ws[:, 0, :], ws_cols[:, :, 0])
+        nc.vector.tensor_copy(ws[:, 1:, :].rearrange("p t m -> p m t"), ws_cols[:, :, 1:])
+        cs = sb.tile([P, PACK, P], U8, name="cs", align_bytes=64)
+        qw = sb.tile([P, S], U32, name="qw", tag="qw_then_cw", align_bytes=64)
         for h in range(2):
             nc.vector.tensor_copy(qw[:, HALF * h : HALF * (h + 1)], xw[:].indirect(entries(offs_t, HALF * h, HALF)))
-        cs_raw = sb.tile([P, C], U8, name="cs_raw", align_bytes=64)
-        nc.vector.tensor_copy(cs_raw[:], xs[:].indirect(cand_t[:]))
-        nc.vector.tensor_copy(cs[:].rearrange("p t m -> p m t"), cs_raw[:].rearrange("p (m t) -> p m t", t=PACK))
+        nc.vector.tensor_copy(cs[:].rearrange("p t m -> p m t"), xs[:].indirect(cand_t[:]))
 
         pieces = [(0, slice(0, HALF), "y_first"), (0, slice(HALF, S), "y_then_s")] + [(t, slice(0, S), f"y{t}") for t in range(1, PACK)]
         y_ps = []
@@ -94,16 +92,13 @@ def tile_picked_candundersend_none_po_kernel(tc, x_words, x_scales, w1_words, w1
             y_ps.append(bank)
 
         y = sb.tile([P, PACK, S], F32, name="y", align_bytes=64)
-        cw = sb.tile([P, PACK, P], U32, name="cw", align_bytes=64)
         for (t, cols, tag), bank in zip(pieces, y_ps):
             if t == 0:
                 nc.scalar.activation(y[:, t, cols], bank[:], COPY, scale=gs_abs[:, t : t + 1])
             else:
                 nc.vector.tensor_scalar(y[:, t, cols], bank[:], gs_abs[:, t : t + 1], None, ALU.mult)
-        for h in range(2):
-            cw_raw = sb.tile([P, S], U32, name=f"cw_raw{h}", tag=("cw_raw", "qw_then_cw_raw")[h], align_bytes=64)
-            nc.vector.tensor_copy(cw_raw[:], xw[:].indirect(entries(cand_t, S * h, S)))
-            nc.vector.tensor_copy(cw[:, :, 64 * h : 64 * (h + 1)].rearrange("p t m -> p m t"), cw_raw[:].rearrange("p (m t) -> p m t", t=PACK))
+        cw = sb.tile([P, PACK, P], U32, name="cw", tag="qw_then_cw", align_bytes=64)
+        nc.vector.tensor_copy(cw[:].rearrange("p t m -> p m t"), xw[:].indirect(cand_t[:]))
 
         s_ps = [ps.tile([P, S], F32, name=f"s_ps{t}", tag=("s0", "s1", "s2", "y_then_s")[t]) for t in range(PACK)]
         ds = [sb.tile([P, S], F32, name=f"ds{t}", align_bytes=64) for t in range(PACK)]

@@ -16,20 +16,33 @@ FP8X4 = mybir.dt.float8_e4m3fn_x4
 FP4X4 = mybir.dt.float4_e2m1fn_x4
 ALU = mybir.AluOpType
 ACT = mybir.ActivationFunctionType
-COPY = ACT.Copy
 
 P = 128
 PACK = 4
-HALF = S // 2
+QUADRANTS = 4
+SCALE_ROWS = 4
 LIST_ROWS = 16
+HALF = S // 2
+QUARTER = S // 4
+X_FIRST = T // 4
+S_SCALE = 0.0625
 
 
 def entries(list_tile, first, count):
     return list_tile[:, first // LIST_ROWS : (first + count) // LIST_ROWS]
 
 
-def tile_picked_candundersend_none_po_kernel(tc, x_words, x_scales, w1_words, w1_scales, gs, offs, n1, n2, cand, n3, out_0, out_1, out_2):
+def scale_rows(tile, dram, q):
+    on_chip = tile[32 * q : 32 * q + SCALE_ROWS, :].bitcast(I32)
+    in_dram = dram[0, SCALE_ROWS * q : SCALE_ROWS * (q + 1), :].bitcast(I32)
+    return on_chip, in_dram
+
+
+def tile_picked_candundersend_none_po_kernel(
+    tc, x_words, x_scales, w1_words, w1_scales, gs, offs, n1, n2, cand, n3, out_0, out_1, out_2
+):
     nc = tc.nc
+    halves = [slice(HALF * h, HALF * (h + 1)) for h in range(2)]
     with ExitStack() as ctx:
         sb = ctx.enter_context(tc.tile_pool(name="sb", bufs=1))
         ps = ctx.enter_context(tc.psum_pool(name="ps", bufs=1))
@@ -48,26 +61,27 @@ def tile_picked_candundersend_none_po_kernel(tc, x_words, x_scales, w1_words, w1
         nc.vector.memset(xs[:, : T // 2].bitcast(I32), 0)
         nc.gpsimd.memset(xs[:, T // 2 :].bitcast(I32), 0)
         nc.vector.memset(ws_raw[:].bitcast(I32), 0)
+
+        x_flat = x_words[0].rearrange("p n t -> p (n t)").bitcast(I32)
+        nc.sync.dma_start(xw[:, :X_FIRST].bitcast(I32), x_flat[:, :X_FIRST])
         nc.sync.dma_start(offs_t[:], offs)
         nc.sync.dma_start(cand_t[:], cand)
+        for q in range(QUADRANTS):
+            nc.sync.dma_start(*scale_rows(xs, x_scales, q))
+        nc.sync.dma_start(xw[:, X_FIRST:].bitcast(I32), x_flat[:, X_FIRST:])
         nc.sync.dma_start(ww_raw[:].bitcast(I32), w1_words[0].bitcast(I32))
-        nc.sync.dma_start(xs[0:4, :].bitcast(I32), x_scales[0, 0:4, :].bitcast(I32))
-        nc.sync.dma_start(xs[32:36, :].bitcast(I32), x_scales[0, 4:8, :].bitcast(I32))
-        nc.sync.dma_start(xs[64:68, :].bitcast(I32), x_scales[0, 8:12, :].bitcast(I32))
-        nc.sync.dma_start(xs[96:100, :].bitcast(I32), x_scales[0, 12:16, :].bitcast(I32))
-        nc.sync.dma_start(xw[:].bitcast(I32), x_words[0].rearrange("p n t -> p (n t)").bitcast(I32))
-        nc.sync.dma_start(ws_raw[0:4, :].bitcast(I32), w1_scales[0, 0:4, :].bitcast(I32))
-        nc.sync.dma_start(ws_raw[32:36, :].bitcast(I32), w1_scales[0, 4:8, :].bitcast(I32))
-        nc.sync.dma_start(ws_raw[64:68, :].bitcast(I32), w1_scales[0, 8:12, :].bitcast(I32))
-        nc.sync.dma_start(ws_raw[96:100, :].bitcast(I32), w1_scales[0, 12:16, :].bitcast(I32))
-        nc.sync.dma_start(gs_t[:], gs.rearrange("(p t) o -> p (t o)", t=PACK))
+        for q in range(QUADRANTS):
+            nc.sync.dma_start(*scale_rows(ws_raw, w1_scales, q))
         nc.sync.dma_start(n1_t[:], n1)
         nc.sync.dma_start(n2_t[:], n2)
         nc.sync.dma_start(n3_t[:], n3)
+        nc.gpsimd.dma_start(gs_t[:], gs.rearrange("(p t) o -> p (t o)", t=PACK))
 
         ww = sb.tile([P, PACK, P], U16, name="ww", align_bytes=64)
         ws = sb.tile([P, PACK, P], U8, name="ws", align_bytes=64)
-        nc.scalar.copy(ww[:].rearrange("p t m -> p m t"), ww_raw[:].rearrange("p (m t) -> p m t", t=PACK))
+        ww_cols = ww_raw[:].rearrange("p (m t) -> p m t", t=PACK)
+        nc.scalar.copy(ww[:, 0, :], ww_cols[:, :, 0])
+        nc.scalar.copy(ww[:, 1:, :].rearrange("p t m -> p m t"), ww_cols[:, :, 1:])
         gs_abs = sb.tile([P, PACK], F32, name="gs_abs")
         gs_sign = sb.tile([P, PACK], BF16, name="gs_sign")
         nc.scalar.activation(gs_abs[:], gs_t[:], ACT.Abs)
@@ -79,22 +93,30 @@ def tile_picked_candundersend_none_po_kernel(tc, x_words, x_scales, w1_words, w1
         nc.vector.tensor_copy(ws[:, 1:, :].rearrange("p t m -> p m t"), ws_cols[:, :, 1:])
         cs = sb.tile([P, PACK, P], U8, name="cs", align_bytes=64)
         qw = sb.tile([P, S], U32, name="qw", tag="qw_then_cw", align_bytes=64)
-        for h in range(2):
-            nc.vector.tensor_copy(qw[:, HALF * h : HALF * (h + 1)], xw[:].indirect(entries(offs_t, HALF * h, HALF)))
+        for cols in halves:
+            nc.vector.tensor_copy(qw[:, cols], xw[:].indirect(entries(offs_t, cols.start, HALF)))
         nc.vector.tensor_copy(cs[:].rearrange("p t m -> p m t"), xs[:].indirect(cand_t[:]))
 
-        pieces = [(0, slice(0, HALF), "y_first"), (0, slice(HALF, S), "y_then_s")] + [(t, slice(0, S), f"y{t}") for t in range(1, PACK)]
+        y_pieces = [(0, halves[0], "y_first"), (0, halves[1], "y_then_s")]
+        y_pieces = y_pieces + [(t, slice(0, S), f"y{t}") for t in range(1, PACK)]
         y_ps = []
-        for t, cols, tag in pieces:
+        for t, cols, tag in y_pieces:
             bank = ps.tile([P, cols.stop - cols.start], F32, name=f"y_ps{t}_{cols.start}", tag=tag)
-            nc.tensor.matmul_mx(bank[:], lhsT=ww[:, t, :].bitcast(FP4X4), lhsT_scale=ws[:, t, :],
-                                rhs=qw[:, cols].bitcast(FP8X4), rhs_scale=qs[:, cols], start=True, stop=True)
+            nc.tensor.matmul_mx(
+                bank[:],
+                lhsT=ww[:, t, :].bitcast(FP4X4),
+                lhsT_scale=ws[:, t, :],
+                rhs=qw[:, cols].bitcast(FP8X4),
+                rhs_scale=qs[:, cols],
+                start=True,
+                stop=True,
+            )
             y_ps.append(bank)
 
         y = sb.tile([P, PACK, S], F32, name="y", align_bytes=64)
-        for (t, cols, tag), bank in zip(pieces, y_ps):
+        for (t, cols, tag), bank in zip(y_pieces, y_ps):
             if t == 0:
-                nc.scalar.activation(y[:, t, cols], bank[:], COPY, scale=gs_abs[:, t : t + 1])
+                nc.scalar.activation(y[:, t, cols], bank[:], ACT.Copy, scale=gs_abs[:, t : t + 1])
             else:
                 nc.vector.tensor_scalar(y[:, t, cols], bank[:], gs_abs[:, t : t + 1], None, ALU.mult)
         cw = sb.tile([P, PACK, P], U32, name="cw", tag="qw_then_cw", align_bytes=64)
@@ -103,17 +125,17 @@ def tile_picked_candundersend_none_po_kernel(tc, x_words, x_scales, w1_words, w1
         s_ps = [ps.tile([P, S], F32, name=f"s_ps{t}", tag=("s0", "s1", "s2", "y_then_s")[t]) for t in range(PACK)]
         ds = [sb.tile([P, S], F32, name=f"ds{t}", align_bytes=64) for t in range(PACK)]
         rl = sb.tile([P, PACK, S], F32, name="rl", align_bytes=64)
-        sign_b = gs_sign[:].unsqueeze(1).to_broadcast([P, HALF, PACK])
+        sign_cols = gs_sign[:].unsqueeze(1).to_broadcast([P, QUARTER, PACK])
         g1 = sb.tile([P, PACK, HALF], F32, name="g1", align_bytes=64)
         g2 = sb.tile([P, PACK, HALF], F32, name="g2", align_bytes=64)
 
-        def gathers(h):
+        def gather_neighbours(h):
             for t in range(PACK):
-                nc.scalar.activation(g1[:, t, :], y[:, t, :].indirect(entries(n1_t, HALF * h, HALF)), COPY)
-                nc.scalar.activation(g2[:, t, :], y[:, t, :].indirect(entries(n2_t, HALF * h, HALF)), COPY)
+                nc.scalar.activation(g1[:, t, :], y[:, t, :].indirect(entries(n1_t, HALF * h, HALF)), ACT.Copy)
+                nc.scalar.activation(g2[:, t, :], y[:, t, :].indirect(entries(n2_t, HALF * h, HALF)), ACT.Copy)
 
-        def make_z(h):
-            cols = slice(HALF * h, HALF * (h + 1))
+        def score(h):
+            cols = halves[h]
             low = sb.tile([P, PACK, HALF], F32, name=f"low{h}", tag=("low", "zb_then_low")[h], align_bytes=64)
             za = sb.tile([P, HALF * PACK], BF16, name=f"za{h}", tag=("za", "zw_then_za")[h], align_bytes=64)
             zb = sb.tile([P, HALF * PACK], BF16, name=f"zb{h}", tag=("zb_then_low", "zb")[h], align_bytes=64)
@@ -121,47 +143,70 @@ def tile_picked_candundersend_none_po_kernel(tc, x_words, x_scales, w1_words, w1
             zs = sb.tile([P, HALF], U8, name=f"zs{h}", align_bytes=64)
             for planes in (slice(0, PACK - 1), slice(PACK - 1, PACK)):
                 nc.vector.tensor_tensor(low[:, planes, :], g1[:, planes, :], g2[:, planes, :], ALU.min)
-            nc.vector.tensor_tensor(za[:].rearrange("p (c i t) -> p c t i", i=2, t=PACK),
-                                    y[:, :, cols].rearrange("p t (c i) -> p c t i", i=2),
-                                    low[:].rearrange("p t (c i) -> p c t i", i=2), ALU.subtract)
-            nc.vector.tensor_tensor(zb[:].rearrange("p (j t) -> p j t", t=PACK), za[:].rearrange("p (j t) -> p j t", t=PACK), sign_b, ALU.mult)
-            nc.vector.quantize_mx(zw[:].bitcast(FP8X4), zs[:], zb[:])
+            quarters = [slice(QUARTER * u, QUARTER * (u + 1)) for u in range(2)]
+            interleaved = [slice(PACK * part.start, PACK * part.stop) for part in quarters]
+            for part, wide in zip(quarters, interleaved):
+                nc.vector.tensor_tensor(
+                    za[:, wide].rearrange("p (c i t) -> p c t i", i=2, t=PACK),
+                    y[:, :, cols][:, :, part].rearrange("p t (c i) -> p c t i", i=2),
+                    low[:, :, part].rearrange("p t (c i) -> p c t i", i=2),
+                    ALU.subtract,
+                )
+            for wide in interleaved:
+                nc.vector.tensor_tensor(
+                    zb[:, wide].rearrange("p (j t) -> p j t", t=PACK),
+                    za[:, wide].rearrange("p (j t) -> p j t", t=PACK),
+                    sign_cols,
+                    ALU.mult,
+                )
+            for part, wide in zip(quarters, interleaved):
+                nc.vector.quantize_mx(zw[:, part].bitcast(FP8X4), zs[:, part], zb[:, wide])
             for t in range(PACK):
-                nc.tensor.matmul_mx(s_ps[t][:, cols], lhsT=cw[:, t, :].bitcast(FP8X4), lhsT_scale=cs[:, t, :],
-                                    rhs=zw[:].bitcast(FP8X4), rhs_scale=zs[:], start=True, stop=True)
+                nc.tensor.matmul_mx(
+                    s_ps[t][:, cols],
+                    lhsT=cw[:, t, :].bitcast(FP8X4),
+                    lhsT_scale=cs[:, t, :],
+                    rhs=zw[:].bitcast(FP8X4),
+                    rhs_scale=zs[:],
+                    start=True,
+                    stop=True,
+                )
             for t in range(PACK):
-                nc.vector.tensor_scalar(rl[:, t, cols], s_ps[t][:, cols], 0.0625, 0.0, ALU.mult, ALU.max)
+                nc.vector.tensor_scalar(rl[:, t, cols], s_ps[t][:, cols], S_SCALE, 0.0, ALU.mult, ALU.max)
 
         def scatter(h, t):
-            cols = slice(HALF * h, HALF * (h + 1))
-            nc.scalar.activation(ds[t][:].indirect(entries(n3_t, HALF * h, HALF)), rl[:, t, cols], COPY)
+            nc.scalar.activation(ds[t][:].indirect(entries(n3_t, HALF * h, HALF)), rl[:, t, halves[h]], ACT.Copy)
 
         res = sb.tile([P, PACK, S], F32, name="res", align_bytes=64)
         rb = sb.tile([P, S * PACK], BF16, name="rb", align_bytes=64)
         ow = sb.tile([P, S], U32, name="ow", align_bytes=64)
         osc = sb.tile([P, S], U8, name="osc", align_bytes=64)
         out_rows = out_0.rearrange("(p t) j -> p t j", t=PACK)
+        rb_cols = rb[:].rearrange("p (j t) -> p j t", t=PACK)
 
-        gathers(0)
-        make_z(0)
-        gathers(1)
+        gather_neighbours(0)
+        score(0)
+        gather_neighbours(1)
         for t in range(PACK):
             scatter(0, t)
-        make_z(1)
-        rb_cols = rb[:].rearrange("p (j t) -> p j t", t=PACK)
-        halves = [slice(HALF * h, HALF * (h + 1)) for h in range(2)]
+        score(1)
         for t in range(PACK):
             scatter(1, t)
-            pieces = halves if t == PACK - 1 else [slice(0, S)]
-            for cols in pieces:
-                nc.vector.scalar_tensor_tensor(res[:, t, cols], s_ps[t][:, cols], -0.03125, ds[t][:, cols], ALU.mult, ALU.add)
+            out_pieces = halves if t == PACK - 1 else [slice(0, S)]
+            for cols in out_pieces:
+                nc.vector.scalar_tensor_tensor(
+                    res[:, t, cols], s_ps[t][:, cols], -0.5 * S_SCALE, ds[t][:, cols], ALU.mult, ALU.add
+                )
             nc.sync.dma_start(out_rows[:, t, :], res[:, t, :])
             if t % 2 == 1:
-                for cols in pieces:
-                    nc.vector.tensor_copy(rb_cols[:, cols, t - 1 : t + 1], res[:, t - 1 : t + 1, cols].rearrange("p t j -> p j t"))
-        for h, cols in enumerate(halves):
-            nc.vector.quantize_mx(ow[:, cols].bitcast(FP8X4), osc[:, cols], rb[:, PACK * HALF * h : PACK * HALF * (h + 1)])
+                for cols in out_pieces:
+                    nc.vector.tensor_copy(
+                        rb_cols[:, cols, t - 1 : t + 1], res[:, t - 1 : t + 1, cols].rearrange("p t j -> p j t")
+                    )
+        for cols in halves:
+            nc.vector.quantize_mx(ow[:, cols].bitcast(FP8X4), osc[:, cols], rb[:, PACK * cols.start : PACK * cols.stop])
+
         nc.scalar.dma_start(out_1[0].rearrange("p n t -> p (n t)").bitcast(I32), ow[:].bitcast(I32))
-        for q in range(4):
-            eng = nc.sync if q % 2 == 0 else nc.scalar
-            eng.dma_start(out_2[0, 4 * q : 4 * q + 4, :].bitcast(I32), osc[32 * q : 32 * q + 4, :].bitcast(I32))
+        for q in range(QUADRANTS):
+            on_chip, in_dram = scale_rows(osc, out_2, q)
+            (nc.sync, nc.scalar)[q % 2].dma_start(in_dram, on_chip)

from contextlib import ExitStack

import concourse.mybir as mybir

K, T, S, H, C = 512, 2048, 256, 512, 512
FLOPS = 2 * K * H * S + 2 * K * C * S
BYTES = (K * (S + C) + K * (S + C) // 32) + K * H // 2 + K * H // 32 + 4 * K + C * S * 4 + C * S + C * S // 32

F32 = mybir.dt.float32
BF16 = mybir.dt.bfloat16
I32 = mybir.dt.int32
U32 = mybir.dt.uint32
U16 = mybir.dt.uint16
U8 = mybir.dt.uint8
FP8X4 = mybir.dt.float8_e4m3fn_x4
FP4X4 = mybir.dt.float4_e2m1fn_x4
ALU = mybir.AluOpType
ACT = mybir.ActivationFunctionType

P = 128
PACK = 4
QUADRANTS = 4
SCALE_ROWS = 4
LIST_ROWS = 16
HALF = S // 2
QUARTER = S // 4
X_FIRST = T // 4
S_SCALE = 0.0625


def entries(list_tile, first, count):
    return list_tile[:, first // LIST_ROWS : (first + count) // LIST_ROWS]


def scale_rows(tile, dram, q):
    on_chip = tile[32 * q : 32 * q + SCALE_ROWS, :].bitcast(I32)
    in_dram = dram[0, SCALE_ROWS * q : SCALE_ROWS * (q + 1), :].bitcast(I32)
    return on_chip, in_dram


def tile_picked_candundersend_none_po_kernel(
    tc, x_words, x_scales, w1_words, w1_scales, gs, offs, n1, n2, cand, n3, out_0, out_1, out_2
):
    nc = tc.nc
    halves = [slice(HALF * h, HALF * (h + 1)) for h in range(2)]
    with ExitStack() as ctx:
        sb = ctx.enter_context(tc.tile_pool(name="sb", bufs=1))
        ps = ctx.enter_context(tc.psum_pool(name="ps", bufs=1))

        offs_t = sb.tile([P, S // LIST_ROWS], U16, name="offs_t")
        cand_t = sb.tile([P, C // LIST_ROWS], U16, name="cand_t")
        n1_t = sb.tile([P, S // LIST_ROWS], U16, name="n1_t")
        n2_t = sb.tile([P, S // LIST_ROWS], U16, name="n2_t")
        n3_t = sb.tile([P, S // LIST_ROWS], U16, name="n3_t")
        xw = sb.tile([P, T], U32, name="xw", align_bytes=64)
        xs = sb.tile([P, T], U8, name="xs", align_bytes=64)
        ww_raw = sb.tile([P, H], U16, name="ww_raw", align_bytes=64)
        ws_raw = sb.tile([P, H], U8, name="ws_raw", align_bytes=64)
        gs_t = sb.tile([P, PACK], F32, name="gs_t")

        nc.vector.memset(xs[:, : T // 2].bitcast(I32), 0)
        nc.gpsimd.memset(xs[:, T // 2 :].bitcast(I32), 0)
        nc.vector.memset(ws_raw[:].bitcast(I32), 0)

        x_flat = x_words[0].rearrange("p n t -> p (n t)").bitcast(I32)
        nc.sync.dma_start(xw[:, :X_FIRST].bitcast(I32), x_flat[:, :X_FIRST])
        nc.sync.dma_start(offs_t[:], offs)
        nc.sync.dma_start(cand_t[:], cand)
        for q in range(QUADRANTS):
            nc.sync.dma_start(*scale_rows(xs, x_scales, q))
        nc.sync.dma_start(xw[:, X_FIRST:].bitcast(I32), x_flat[:, X_FIRST:])
        nc.sync.dma_start(ww_raw[:].bitcast(I32), w1_words[0].bitcast(I32))
        for q in range(QUADRANTS):
            nc.sync.dma_start(*scale_rows(ws_raw, w1_scales, q))
        nc.sync.dma_start(n1_t[:], n1)
        nc.sync.dma_start(n2_t[:], n2)
        nc.sync.dma_start(n3_t[:], n3)
        nc.gpsimd.dma_start(gs_t[:], gs.rearrange("(p t) o -> p (t o)", t=PACK))

        ww = sb.tile([P, PACK, P], U16, name="ww", align_bytes=64)
        ws = sb.tile([P, PACK, P], U8, name="ws", align_bytes=64)
        ww_cols = ww_raw[:].rearrange("p (m t) -> p m t", t=PACK)
        nc.scalar.copy(ww[:, 0, :], ww_cols[:, :, 0])
        nc.scalar.copy(ww[:, 1:, :].rearrange("p t m -> p m t"), ww_cols[:, :, 1:])
        gs_abs = sb.tile([P, PACK], F32, name="gs_abs")
        gs_sign = sb.tile([P, PACK], BF16, name="gs_sign")
        nc.scalar.activation(gs_abs[:], gs_t[:], ACT.Abs)
        nc.scalar.activation(gs_sign[:], gs_t[:], ACT.Sign)
        qs = sb.tile([P, S], U8, name="qs", align_bytes=64)
        nc.vector.tensor_copy(qs[:], xs[:].indirect(offs_t[:]))
        ws_cols = ws_raw[:].rearrange("p (m t) -> p m t", t=PACK)
        nc.vector.tensor_copy(ws[:, 0, :], ws_cols[:, :, 0])
        nc.vector.tensor_copy(ws[:, 1:, :].rearrange("p t m -> p m t"), ws_cols[:, :, 1:])
        cs = sb.tile([P, PACK, P], U8, name="cs", align_bytes=64)
        qw = sb.tile([P, S], U32, name="qw", tag="qw_then_cw", align_bytes=64)
        for cols in halves:
            nc.vector.tensor_copy(qw[:, cols], xw[:].indirect(entries(offs_t, cols.start, HALF)))
        nc.vector.tensor_copy(cs[:].rearrange("p t m -> p m t"), xs[:].indirect(cand_t[:]))

        y_pieces = [(0, halves[0], "y_first"), (0, halves[1], "y_then_s")]
        y_pieces = y_pieces + [(t, slice(0, S), f"y{t}") for t in range(1, PACK)]
        y_ps = []
        for t, cols, tag in y_pieces:
            bank = ps.tile([P, cols.stop - cols.start], F32, name=f"y_ps{t}_{cols.start}", tag=tag)
            nc.tensor.matmul_mx(
                bank[:],
                lhsT=ww[:, t, :].bitcast(FP4X4),
                lhsT_scale=ws[:, t, :],
                rhs=qw[:, cols].bitcast(FP8X4),
                rhs_scale=qs[:, cols],
                start=True,
                stop=True,
            )
            y_ps.append(bank)

        y = sb.tile([P, PACK, S], F32, name="y", align_bytes=64)
        for (t, cols, tag), bank in zip(y_pieces, y_ps):
            if t == 0:
                nc.scalar.activation(y[:, t, cols], bank[:], ACT.Copy, scale=gs_abs[:, t : t + 1])
            else:
                nc.vector.tensor_scalar(y[:, t, cols], bank[:], gs_abs[:, t : t + 1], None, ALU.mult)
        cw = sb.tile([P, PACK, P], U32, name="cw", tag="qw_then_cw", align_bytes=64)
        nc.vector.tensor_copy(cw[:].rearrange("p t m -> p m t"), xw[:].indirect(cand_t[:]))

        s_ps = [ps.tile([P, S], F32, name=f"s_ps{t}", tag=("s0", "s1", "s2", "y_then_s")[t]) for t in range(PACK)]
        ds = [sb.tile([P, S], F32, name=f"ds{t}", align_bytes=64) for t in range(PACK)]
        rl = sb.tile([P, PACK, S], F32, name="rl", align_bytes=64)
        sign_cols = gs_sign[:].unsqueeze(1).to_broadcast([P, QUARTER, PACK])
        g1 = sb.tile([P, PACK, HALF], F32, name="g1", align_bytes=64)
        g2 = sb.tile([P, PACK, HALF], F32, name="g2", align_bytes=64)

        def gather_neighbours(h):
            for t in range(PACK):
                nc.scalar.activation(g1[:, t, :], y[:, t, :].indirect(entries(n1_t, HALF * h, HALF)), ACT.Copy)
                nc.scalar.activation(g2[:, t, :], y[:, t, :].indirect(entries(n2_t, HALF * h, HALF)), ACT.Copy)

        def score(h):
            cols = halves[h]
            low = sb.tile([P, PACK, HALF], F32, name=f"low{h}", tag=("low", "zb_then_low")[h], align_bytes=64)
            za = sb.tile([P, HALF * PACK], BF16, name=f"za{h}", tag=("za", "zw_then_za")[h], align_bytes=64)
            zb = sb.tile([P, HALF * PACK], BF16, name=f"zb{h}", tag=("zb_then_low", "zb")[h], align_bytes=64)
            zw = sb.tile([P, HALF], U32, name=f"zw{h}", tag=("zw_then_za", "zw")[h], align_bytes=64)
            zs = sb.tile([P, HALF], U8, name=f"zs{h}", align_bytes=64)
            for planes in (slice(0, PACK - 1), slice(PACK - 1, PACK)):
                nc.vector.tensor_tensor(low[:, planes, :], g1[:, planes, :], g2[:, planes, :], ALU.min)
            quarters = [slice(QUARTER * u, QUARTER * (u + 1)) for u in range(2)]
            interleaved = [slice(PACK * part.start, PACK * part.stop) for part in quarters]
            for part, wide in zip(quarters, interleaved):
                nc.vector.tensor_tensor(
                    za[:, wide].rearrange("p (c i t) -> p c t i", i=2, t=PACK),
                    y[:, :, cols][:, :, part].rearrange("p t (c i) -> p c t i", i=2),
                    low[:, :, part].rearrange("p t (c i) -> p c t i", i=2),
                    ALU.subtract,
                )
            for wide in interleaved:
                nc.vector.tensor_tensor(
                    zb[:, wide].rearrange("p (j t) -> p j t", t=PACK),
                    za[:, wide].rearrange("p (j t) -> p j t", t=PACK),
                    sign_cols,
                    ALU.mult,
                )
            for part, wide in zip(quarters, interleaved):
                nc.vector.quantize_mx(zw[:, part].bitcast(FP8X4), zs[:, part], zb[:, wide])
            for t in range(PACK):
                nc.tensor.matmul_mx(
                    s_ps[t][:, cols],
                    lhsT=cw[:, t, :].bitcast(FP8X4),
                    lhsT_scale=cs[:, t, :],
                    rhs=zw[:].bitcast(FP8X4),
                    rhs_scale=zs[:],
                    start=True,
                    stop=True,
                )
            for t in range(PACK):
                nc.vector.tensor_scalar(rl[:, t, cols], s_ps[t][:, cols], S_SCALE, 0.0, ALU.mult, ALU.max)

        def scatter(h, t):
            nc.scalar.activation(ds[t][:].indirect(entries(n3_t, HALF * h, HALF)), rl[:, t, halves[h]], ACT.Copy)

        res = sb.tile([P, PACK, S], F32, name="res", align_bytes=64)
        rb = sb.tile([P, S * PACK], BF16, name="rb", align_bytes=64)
        ow = sb.tile([P, S], U32, name="ow", align_bytes=64)
        osc = sb.tile([P, S], U8, name="osc", align_bytes=64)
        out_rows = out_0.rearrange("(p t) j -> p t j", t=PACK)
        rb_cols = rb[:].rearrange("p (j t) -> p j t", t=PACK)

        gather_neighbours(0)
        score(0)
        gather_neighbours(1)
        for t in range(PACK):
            scatter(0, t)
        score(1)
        for t in range(PACK):
            scatter(1, t)
            out_pieces = halves if t == PACK - 1 else [slice(0, S)]
            for cols in out_pieces:
                nc.vector.scalar_tensor_tensor(
                    res[:, t, cols], s_ps[t][:, cols], -0.5 * S_SCALE, ds[t][:, cols], ALU.mult, ALU.add
                )
            nc.sync.dma_start(out_rows[:, t, :], res[:, t, :])
            if t % 2 == 1:
                for cols in out_pieces:
                    nc.vector.tensor_copy(
                        rb_cols[:, cols, t - 1 : t + 1], res[:, t - 1 : t + 1, cols].rearrange("p t j -> p j t")
                    )
        for cols in halves:
            nc.vector.quantize_mx(ow[:, cols].bitcast(FP8X4), osc[:, cols], rb[:, PACK * cols.start : PACK * cols.stop])

        nc.scalar.dma_start(out_1[0].rearrange("p n t -> p (n t)").bitcast(I32), ow[:].bitcast(I32))
        for q in range(QUADRANTS):
            on_chip, in_dram = scale_rows(osc, out_2, q)
            (nc.sync, nc.scalar)[q % 2].dma_start(in_dram, on_chip)
